import numpy as np
import ml_dtypes


def mxq(x, axis, fmt="e4m3"):
    dtype, down = {"e4m3": (ml_dtypes.float8_e4m3fn, 7), "e5m2": (ml_dtypes.float8_e5m2, 14)}[fmt]
    v = np.moveaxis(np.asarray(x, np.float32).astype(ml_dtypes.bfloat16).astype(np.float64), axis, -1)
    blocks = v.reshape(v.shape[:-1] + (-1, 32))
    amax = np.abs(blocks).max(-1, keepdims=True)
    byte = np.maximum(np.where(amax > 0, np.frexp(amax)[1] - 1 + 127, 0) - down, 1)
    scale = np.exp2(byte - 127.0)
    codes = (blocks / scale).astype(np.float32).astype(dtype).astype(np.float64)
    return np.moveaxis((codes * scale).reshape(v.shape), -1, axis)


WIDE = False


def mx_kscale(k):
    if not WIDE:
        return np.ones(k)
    levels = np.array([10, -10, 5, -5, 0])
    if k % 512:
        return np.exp2(np.random.permutation(np.resize(levels, k // 32))).repeat(32)
    a = np.empty((k // 512, 16))
    for p in range(k // 512):
        a[p, :8] = np.random.permutation(np.resize(levels, 8))
        for g in range(8):
            far = levels[np.abs(levels - a[p, g]) >= 10]
            a[p, g + 8] = far[np.random.randint(len(far))]
    return np.exp2(a.ravel()).repeat(32)


def f64(x):
    return np.asarray(x).astype(np.float64)


def striped8(idx):
    return np.concatenate([v.reshape(-1, 16).T for v in idx]).astype(np.uint16)


def unstriped8(offs):
    return np.stack([offs[16 * g:16 * g + 16].T.reshape(-1) for g in range(8)]).astype(np.int64)


E2M1 = np.array([0.0, 0.5, 1.0, 1.5, 2.0, 3.0, 4.0, 6.0, -0.0, -0.5, -1.0, -1.5, -2.0, -3.0, -4.0, -6.0])


def pack_weight(w, fmt):
    k, n = w.shape
    w = f64(np.asarray(w, np.float32).astype(ml_dtypes.bfloat16)).reshape(k // 32, 32, n)
    amax = np.abs(w).max(1)
    if fmt == "e4m3":
        byte = np.frexp(amax)[1] - 1 + 127 - 7
    else:
        mant, ex = np.frexp(amax / 6.0)
        byte = np.where(mant > 0.5, ex, ex - 1) + 127
    byte = np.clip(np.where(amax > 0, byte, 1), 1, 254)
    scaled = (w * np.exp2(127.0 - byte)[:, None, :]).reshape(k, n).astype(np.float32)
    by_word = np.ascontiguousarray(scaled.reshape(k // 512, 128, 4, n).transpose(0, 1, 3, 2))
    if fmt == "e4m3":
        words = by_word.astype(ml_dtypes.float8_e4m3fn).view(np.uint8)
    else:
        c = by_word.astype(ml_dtypes.float4_e2m1fn).view(np.uint8) & 0xF
        words = (c[..., 0::2] | (c[..., 1::2] << 4)).reshape(k // 512, 128, 2 * n)
    return np.ascontiguousarray(words), np.ascontiguousarray(byte.astype(np.uint8).reshape(k // 512, 16, n))


def unpack_weight(words, scales, fmt):
    g, _, n = scales.shape
    words = np.ascontiguousarray(words).reshape(g, 128, n, -1)
    if fmt == "e4m3":
        vals = words.view(ml_dtypes.float8_e4m3fn).astype(np.float64)
    else:
        nib = np.empty((g, 128, n, 4), np.uint8)
        nib[..., 0::2] = words & 0xF
        nib[..., 1::2] = words >> 4
        vals = E2M1[nib]
    vals = vals * np.repeat(np.exp2(scales.astype(np.float64) - 127.0), 8, axis=1)[..., None]
    return vals.transpose(0, 1, 3, 2).reshape(g * 512, n)


K, M, T, S = 1536, 256, 1024, 512


def setup_inputs():
    n = np.random.standard_normal
    s = mx_kscale(K)[:, None]
    s2 = mx_kscale(512)[:, None]
    p_w4 = pack_weight(n((K, M)) / np.sqrt(K) / s, "e2m1")
    return {
        "xT": (n((K, T)) * s).astype(np.float32),
        "w4_words": p_w4[0],
        "w4_scales": p_w4[1],
        "c": (n((512, S)) * s2).astype(np.float32),
        "u": (n((512, M)) / np.sqrt(512) / s2).astype(np.float32),
        "wgt": np.repeat(np.random.uniform(0.5, 2.0, (8, S)), 16, axis=0).astype(np.float32),
        "wgo": np.repeat(np.random.uniform(0.5, 2.0, (8, S)), 16, axis=0).astype(np.float32),
        "offs": striped8(np.stack([np.random.permutation(T)[:S] for _ in range(8)])),
        "offs2": striped8(np.stack([np.random.permutation(T)[:S] for _ in range(8)])),
    }


def reference(xT, w4_words, w4_scales, c, u, wgt, wgo, offs, offs2):
    idx = unstriped8(offs)
    group = np.arange(K) % 512 // 64
    xg = f64(wgt)[np.arange(K) // 4 % 128] * f64(xT)[np.arange(K)[:, None], idx[group]]
    xT_ = mxq(xg, 0, "e4m3")
    w4_ = unpack_weight(w4_words, w4_scales, "e2m1")
    c_ = mxq(f64(c), 0, "e4m3")
    u_ = mxq(f64(u), 0, "e4m3")
    y = w4_.T @ xT_ + u_.T @ c_
    place = unstriped8(offs2)[np.arange(M) % 128 // 16]
    out = np.zeros((M, T))
    out[np.arange(M)[:, None], place] = f64(wgo)[np.arange(M) % 128] * (y)
    return out

@@ -1,0 +1,191 @@
+from contextlib import ExitStack
+
+import concourse.mybir as mybir
+
+K, M, T, S = 1536, 256, 1024, 512
+L = 512
+FLOPS = 2 * (K + L) * M * S
+
+F32 = mybir.dt.float32
+BF16 = mybir.dt.bfloat16
+I32 = mybir.dt.int32
+U32 = mybir.dt.uint32
+U16 = mybir.dt.uint16
+U8 = mybir.dt.uint8
+FP8X4 = mybir.dt.float8_e4m3fn_x4
+FP4X4 = mybir.dt.float4_e2m1fn_x4
+MULT = mybir.AluOpType.mult
+
+P = 128
+PACK = 4
+K_PASS = P * PACK
+PASSES = K // K_PASS
+HALF = S // 2
+QUARTER = S // 4
+PER_COL = 16
+
+
+def tile_list_hboth_d_none_kernel(tc, xT, w4_words, w4_scales, c, u, wgt, wgo, offs, offs2, out):
+    nc = tc.nc
+    with ExitStack() as ctx:
+        keep = ctx.enter_context(tc.tile_pool(name="keep", bufs=1))
+        psum = ctx.enter_context(tc.psum_pool(name="psum", bufs=1))
+
+        def tile(shape, dtype, name, tag=None):
+            return keep.tile(shape, dtype, name=name, tag=tag or name, align_bytes=64)
+
+        gather_list = keep.tile([P, S // PER_COL], U16, name="gather_list")
+        scatter_list = keep.tile([P, S // PER_COL], U16, name="scatter_list")
+        planes = [[tile([P, T], F32, f"plane{a}_{i}") for i in range(PACK)] for a in range(PASSES)]
+        wgt_sb = [tile([P, HALF], F32, f"wgt{h}") for h in range(2)]
+        wgo_sb = [tile([P, HALF], F32, f"wgo{h}") for h in range(2)]
+        c_raw = [tile([P, PACK, HALF], F32, f"c_raw{h}") for h in range(2)]
+        u_raw = tile([P, PACK, M], F32, "u_raw")
+        w_words = tile([P, PASSES, 2 * M], U8, "w_words")
+        w_scales = tile([P, PASSES, M], U8, "w_scales")
+        placed = [tile([P, T], F32, f"placed{m}") for m in range(M // P)]
+        banks = [[psum.tile([P, QUARTER], F32, name=f"bank{m}_{q}") for q in range(4)] for m in range(M // P)]
+
+        nc.vector.memset(w_scales[:].rearrange("p a n -> p (a n)").bitcast(I32), 0)
+        for m in range(M // P):
+            nc.vector.memset(placed[m][:], 0.0)
+
+        x_planes = xT.rearrange("(a p i) t -> a i p t", p=P, i=PACK)
+        c_rows = c.rearrange("(p i) j -> p i j", i=PACK)
+
+        def load_planes(a, which):
+            for i in which:
+                nc.sync.dma_start(out=planes[a][i][:], in_=x_planes[a, i])
+
+        def half(h):
+            return slice(h * HALF, (h + 1) * HALF)
+
+        nc.sync.dma_start(gather_list[:], offs)
+        nc.sync.dma_start(out=wgt_sb[0][:], in_=wgt[:, half(0)])
+        load_planes(0, [0])
+        nc.sync.dma_start(out=wgt_sb[1][:], in_=wgt[:, half(1)])
+        load_planes(0, [1, 2, 3])
+        load_planes(1, [0, 1])
+        nc.sync.dma_start(out=u_raw[:], in_=u.rearrange("(p i) n -> p i n", i=PACK))
+        load_planes(1, [2, 3])
+        load_planes(2, [0, 1])
+        for quad in range(4):
+            nc.sync.dma_start(
+                out=w_scales[32 * quad : 32 * quad + 4].bitcast(I32),
+                in_=w4_scales[:, 4 * quad : 4 * quad + 4, :].rearrange("a r n -> r a n").bitcast(I32),
+            )
+        nc.sync.dma_start(out=w_words[:].bitcast(I32), in_=w4_words.rearrange("a p b -> p a b").bitcast(I32))
+        nc.sync.dma_start(out=c_raw[0][:], in_=c_rows[:, :, half(0)])
+        load_planes(2, [2, 3])
+        nc.sync.dma_start(scatter_list[:], offs2)
+        nc.sync.dma_start(out=wgo_sb[0][:], in_=wgo[:, half(0)])
+        nc.sync.dma_start(out=c_raw[1][:], in_=c_rows[:, :, half(1)])
+        nc.sync.dma_start(out=wgo_sb[1][:], in_=wgo[:, half(1)])
+
+        def gather(a, i, j0, width, dst):
+            h, j_in = divmod(j0, HALF)
+            picks = gather_list[:, j0 // PER_COL : (j0 + width) // PER_COL]
+            nc.vector.tensor_tensor(dst, planes[a][i][:].indirect(picks), wgt_sb[h][:, j_in : j_in + width], MULT)
+
+        def interleave(raw, width, name):
+            grouped = tile([P, width, PACK], BF16, name + "_grouped")
+            nc.scalar.copy(
+                out=grouped[:].rearrange("p (b e) i -> p b i e", e=4),
+                in_=raw[:].rearrange("p i (b e) -> p b i e", e=4),
+            )
+            return grouped
+
+        def quantise(grouped, width, name, after=None):
+            codes = tile([P, width], U32, name + "_codes", tag=after)
+            scales = tile([P, width], U8, name + "_scales")
+            nc.vector.quantize_mx(
+                out=codes[:].bitcast(FP8X4), scales=scales[:], in_=grouped[:].rearrange("p w i -> p (w i)")
+            )
+            return codes, scales
+
+        def multiply(lhs, rhs, j0, width, start, stop):
+            codes, scales = rhs
+            for q0 in range(0, width, QUARTER):
+                for m in range(M // P):
+                    lhs_codes, lhs_scales = lhs(m)
+                    nc.tensor.matmul_mx(
+                        out=banks[m][(j0 + q0) // QUARTER][:],
+                        lhsT=lhs_codes,
+                        lhsT_scale=lhs_scales,
+                        rhs=codes[:, q0 : q0 + QUARTER].bitcast(FP8X4),
+                        rhs_scale=scales[:, q0 : q0 + QUARTER],
+                        start=start,
+                        stop=stop,
+                    )
+
+        def w4_pass(a):
+            return lambda m: (
+                w_words[:, a, 2 * P * m : 2 * P * (m + 1)].bitcast(FP4X4),
+                w_scales[:, a, P * m : P * (m + 1)],
+            )
+
+        last = PASSES - 1
+        picked = [tile([P, PACK, S], F32, f"picked{a}") for a in range(last)]
+        pieces = [(0, QUARTER), (QUARTER, QUARTER), (HALF, HALF)]
+        picked_last = [tile([P, PACK, w], F32, f"picked_last{j0}") for j0, w in pieces]
+
+        def gather_plane(a, i):
+            if a < last:
+                for h in range(2):
+                    gather(a, i, h * HALF, HALF, picked[a][:, i, half(h)])
+            else:
+                for (j0, w), dst in zip(pieces, picked_last):
+                    gather(a, i, j0, w, dst[:, i, :])
+
+        for i in range(PACK):
+            gather_plane(0, i)
+        grouped0 = interleave(picked[0], S, "xg0")
+        grouped_u = interleave(u_raw, M, "u")
+        gather_plane(1, 0)
+        gather_plane(1, 1)
+        xg0 = quantise(grouped0, S, "xg0", after="plane1_1")
+        gather_plane(1, 2)
+        u_codes, u_scales = quantise(grouped_u, M, "u", after="plane1_2")
+        gather_plane(1, 3)
+        grouped1 = interleave(picked[1], S, "xg1")
+        grouped_c0 = interleave(c_raw[0], HALF, "c0")
+        gather_plane(2, 0)
+        gather_plane(2, 1)
+        xg1 = quantise(grouped1, S, "xg1", after="plane2_1")
+        gather_plane(2, 2)
+        c0 = quantise(grouped_c0, HALF, "c0", after="plane2_2")
+        gather_plane(2, 3)
+
+        def u_pass(m):
+            return u_codes[:, P * m : P * (m + 1)].bitcast(FP8X4), u_scales[:, P * m : P * (m + 1)]
+
+        multiply(w4_pass(0), xg0, 0, S, True, False)
+        multiply(w4_pass(1), xg1, 0, S, False, False)
+        multiply(u_pass, c0, 0, HALF, False, False)
+
+        sums = {}
+
+        def drain(m, h, tag=None):
+            sums[m, h] = tile([P, HALF], F32, f"sums{m}_{h}", tag=tag)
+            for q_in in range(2):
+                nc.scalar.copy(
+                    out=sums[m, h][:, q_in * QUARTER : (q_in + 1) * QUARTER], in_=banks[m][2 * h + q_in][:]
+                )
+
+        def scatter(m, h):
+            places = scatter_list[:, h * HALF // PER_COL : (h + 1) * HALF // PER_COL]
+            nc.vector.tensor_tensor(placed[m][:].indirect(places), sums[m, h][:], wgo_sb[h][:], MULT)
+
+        for (j0, w), raw in zip(pieces, picked_last):
+            name = f"xg_last{j0}"
+            multiply(w4_pass(last), quantise(interleave(raw, w, name), w, name), j0, w, False, j0 < HALF)
+        drain(0, 0)
+        grouped_c1 = interleave(c_raw[1], HALF, "c1")
+        scatter(0, 0)
+        multiply(u_pass, quantise(grouped_c1, HALF, "c1"), HALF, HALF, False, True)
+        drain(1, 0, tag="c_raw1")
+        scatter(1, 0)
+        for m in range(M // P):
+            drain(m, 1)
+            scatter(m, 1)
+            nc.sync.dma_start(out=out[m * P : (m + 1) * P, :], in_=placed[m][:])

@@ -37,7 +37,8 @@ def tile_list_hboth_d_none_kernel(tc, xT, w4_words, w4_scales, c, u, wgt, wgo, o
         gather_list = keep.tile([P, S // PER_COL], U16, name="gather_list")
         scatter_list = keep.tile([P, S // PER_COL], U16, name="scatter_list")
         planes = [[tile([P, T], F32, f"plane{a}_{i}") for i in range(PACK)] for a in range(PASSES)]
-        wgt_sb = [tile([P, HALF], F32, f"wgt{h}") for h in range(2)]
+        wgt_sb = tile([P, S], F32, "wgt_sb")
+        wgt_once = [tile([P, w], F32, f"wgt_once{n}") for n, w in enumerate((HALF, HALF, QUARTER))]
         wgo_sb = [tile([P, HALF], F32, f"wgo{h}") for h in range(2)]
         c_raw = [tile([P, PACK, HALF], F32, f"c_raw{h}") for h in range(2)]
         u_raw = tile([P, PACK, M], F32, "u_raw")
@@ -60,108 +61,98 @@ def tile_list_hboth_d_none_kernel(tc, xT, w4_words, w4_scales, c, u, wgt, wgo, o
         def half(h):
             return slice(h * HALF, (h + 1) * HALF)
 
-        nc.sync.dma_start(gather_list[:], offs)
-        nc.sync.dma_start(out=wgt_sb[0][:], in_=wgt[:, half(0)])
         load_planes(0, [0])
-        nc.sync.dma_start(out=wgt_sb[1][:], in_=wgt[:, half(1)])
+        nc.sync.dma_start(out=wgt_sb[:], in_=wgt)
+        nc.sync.dma_start(gather_list[:], offs)
         load_planes(0, [1, 2, 3])
-        load_planes(1, [0, 1])
+        load_planes(1, [0])
         nc.sync.dma_start(out=u_raw[:], in_=u.rearrange("(p i) n -> p i n", i=PACK))
+        load_planes(1, [1])
+        nc.sync.dma_start(out=c_raw[0][:], in_=c_rows[:, :, half(0)])
         load_planes(1, [2, 3])
-        load_planes(2, [0, 1])
+        load_planes(2, range(PACK))
+        nc.sync.dma_start(out=w_words[:].bitcast(I32), in_=w4_words.rearrange("a p b -> p a b").bitcast(I32))
+        nc.sync.dma_start(out=wgo_sb[0][:], in_=wgo[:, half(0)])
+        nc.sync.dma_start(scatter_list[:], offs2)
+        nc.sync.dma_start(out=c_raw[1][:], in_=c_rows[:, :, half(1)])
+        nc.sync.dma_start(out=wgo_sb[1][:], in_=wgo[:, half(1)])
         for quad in range(4):
-            nc.sync.dma_start(
+            nc.scalar.dma_start(
                 out=w_scales[32 * quad : 32 * quad + 4].bitcast(I32),
                 in_=w4_scales[:, 4 * quad : 4 * quad + 4, :].rearrange("a r n -> r a n").bitcast(I32),
             )
-        nc.sync.dma_start(out=w_words[:].bitcast(I32), in_=w4_words.rearrange("a p b -> p a b").bitcast(I32))
-        nc.sync.dma_start(out=c_raw[0][:], in_=c_rows[:, :, half(0)])
-        load_planes(2, [2, 3])
-        nc.sync.dma_start(scatter_list[:], offs2)
-        nc.sync.dma_start(out=wgo_sb[0][:], in_=wgo[:, half(0)])
-        nc.sync.dma_start(out=c_raw[1][:], in_=c_rows[:, :, half(1)])
-        nc.sync.dma_start(out=wgo_sb[1][:], in_=wgo[:, half(1)])
 
-        def gather(a, i, j0, width, dst):
-            h, j_in = divmod(j0, HALF)
+        for copy in wgt_once:
+            nc.scalar.copy(out=copy[:], in_=wgt_sb[:, : copy.shape[1]])
+
+        def gather(a, i, j0, width, dst, weights=None):
+            weights = wgt_sb[:, j0 : j0 + width] if weights is None else weights[:]
             picks = gather_list[:, j0 // PER_COL : (j0 + width) // PER_COL]
-            nc.vector.tensor_tensor(dst, planes[a][i][:].indirect(picks), wgt_sb[h][:, j_in : j_in + width], MULT)
+            nc.vector.tensor_tensor(dst, planes[a][i][:].indirect(picks), weights, MULT)
+
+        def interleave_into(copy, grouped, raw):
+            copy(out=grouped.rearrange("p (b e) i -> p b i e", e=4), in_=raw.rearrange("p i (b e) -> p b i e", e=4))
 
         def interleave(raw, width, name):
             grouped = tile([P, width, PACK], BF16, name + "_grouped")
-            nc.scalar.copy(
-                out=grouped[:].rearrange("p (b e) i -> p b i e", e=4),
-                in_=raw[:].rearrange("p i (b e) -> p b i e", e=4),
-            )
+            interleave_into(nc.scalar.copy, grouped[:], raw)
             return grouped
 
-        def quantise(grouped, width, name, after=None):
-            codes = tile([P, width], U32, name + "_codes", tag=after)
-            scales = tile([P, width], U8, name + "_scales")
-            nc.vector.quantize_mx(
-                out=codes[:].bitcast(FP8X4), scales=scales[:], in_=grouped[:].rearrange("p w i -> p (w i)")
-            )
-            return codes, scales
+        def quantise(grouped, codes, name):
+            scales = tile([P, codes.shape[1]], U8, name + "_scales")
+            nc.vector.quantize_mx(out=codes.bitcast(FP8X4), scales=scales[:], in_=grouped.rearrange("p w i -> p (w i)"))
+            return [
+                (codes[:, q0 : q0 + QUARTER].bitcast(FP8X4), scales[:, q0 : q0 + QUARTER])
+                for q0 in range(0, codes.shape[1], QUARTER)
+            ]
 
-        def multiply(lhs, rhs, j0, width, start, stop):
-            codes, scales = rhs
-            for q0 in range(0, width, QUARTER):
-                for m in range(M // P):
-                    lhs_codes, lhs_scales = lhs(m)
-                    nc.tensor.matmul_mx(
-                        out=banks[m][(j0 + q0) // QUARTER][:],
-                        lhsT=lhs_codes,
-                        lhsT_scale=lhs_scales,
-                        rhs=codes[:, q0 : q0 + QUARTER].bitcast(FP8X4),
-                        rhs_scale=scales[:, q0 : q0 + QUARTER],
-                        start=start,
-                        stop=stop,
-                    )
-
-        def w4_pass(a):
-            return lambda m: (
-                w_words[:, a, 2 * P * m : 2 * P * (m + 1)].bitcast(FP4X4),
-                w_scales[:, a, P * m : P * (m + 1)],
+        def multiply(m, q, lhs, rhs, start=False, stop=False):
+            nc.tensor.matmul_mx(
+                out=banks[m][q][:], lhsT=lhs[0], lhsT_scale=lhs[1], rhs=rhs[0], rhs_scale=rhs[1], start=start, stop=stop
             )
+
+        def w4(a, m):
+            return w_words[:, a, 2 * P * m : 2 * P * (m + 1)].bitcast(FP4X4), w_scales[:, a, P * m : P * (m + 1)]
 
         last = PASSES - 1
         picked = [tile([P, PACK, S], F32, f"picked{a}") for a in range(last)]
-        pieces = [(0, QUARTER), (QUARTER, QUARTER), (HALF, HALF)]
-        picked_last = [tile([P, PACK, w], F32, f"picked_last{j0}") for j0, w in pieces]
-
-        def gather_plane(a, i):
-            if a < last:
-                for h in range(2):
-                    gather(a, i, h * HALF, HALF, picked[a][:, i, half(h)])
-            else:
-                for (j0, w), dst in zip(pieces, picked_last):
-                    gather(a, i, j0, w, dst[:, i, :])
+        picked_last = [tile([P, PACK, HALF], F32, f"picked_last{h}") for h in range(2)]
 
         for i in range(PACK):
-            gather_plane(0, i)
-        grouped0 = interleave(picked[0], S, "xg0")
-        grouped_u = interleave(u_raw, M, "u")
-        gather_plane(1, 0)
-        gather_plane(1, 1)
-        xg0 = quantise(grouped0, S, "xg0", after="plane1_1")
-        gather_plane(1, 2)
-        u_codes, u_scales = quantise(grouped_u, M, "u", after="plane1_2")
-        gather_plane(1, 3)
-        grouped1 = interleave(picked[1], S, "xg1")
-        grouped_c0 = interleave(c_raw[0], HALF, "c0")
-        gather_plane(2, 0)
-        gather_plane(2, 1)
-        xg1 = quantise(grouped1, S, "xg1", after="plane2_1")
-        gather_plane(2, 2)
-        c0 = quantise(grouped_c0, HALF, "c0", after="plane2_2")
-        gather_plane(2, 3)
+            for h in range(2):
+                gather(0, i, h * HALF, HALF, picked[0][:, i, half(h)])
+        grouped0 = interleave(picked[0][:], S, "xg0")
+        grouped_u = interleave(u_raw[:], M, "u")
+        for i in range(PACK):
+            gather(1, i, 0, HALF, picked[1][:, i, half(0)], wgt_once[i - 1] if i in (1, 2) else None)
+            gather(1, i, HALF, HALF, picked[1][:, i, half(1)])
+            if i == 1:
+                codes0 = tile([P, S + M], U32, "codes0", tag="wgt_once0")
+                xg0 = quantise(grouped0[:], codes0[:, :S], "xg0")
+                u_mx = quantise(grouped_u[:], codes0[:, S:], "u")
+            if i == 2:
+                codes_c0 = tile([P, HALF], U32, "codes_c0", tag="wgt_once1")
+                c_mx = quantise(interleave(c_raw[0][:], HALF, "c0")[:], codes_c0[:], "c0")
+        grouped1 = interleave(picked[1][:], S, "xg1")
+        for i in range(PACK - 1):
+            for h in range(2):
+                gather(last, i, h * HALF, HALF, picked_last[h][:, i, :])
+        gather(last, 3, 0, QUARTER, picked_last[0][:, 3, :QUARTER], wgt_once[2])
+        gather(last, 3, QUARTER, QUARTER, picked_last[0][:, 3, QUARTER:])
+        gather(last, 3, HALF, HALF, picked_last[1][:, 3, :])
 
-        def u_pass(m):
-            return u_codes[:, P * m : P * (m + 1)].bitcast(FP8X4), u_scales[:, P * m : P * (m + 1)]
-
-        multiply(w4_pass(0), xg0, 0, S, True, False)
-        multiply(w4_pass(1), xg1, 0, S, False, False)
-        multiply(u_pass, c0, 0, HALF, False, False)
+        grouped_h0 = tile([P, HALF, PACK], BF16, "grouped_h0")
+        interleave_into(nc.scalar.copy, grouped_h0[:, :QUARTER, :], picked_last[0][:, :, :QUARTER])
+        interleave_into(nc.vector.tensor_copy, grouped_h0[:, QUARTER:, :], picked_last[0][:, :, QUARTER:])
+        grouped_h1 = interleave(picked_last[1][:], HALF, "xg2_h1")
+        codes2 = tile([P, S], U32, "codes2")
+        codes1_h0 = tile([P, HALF], U32, "codes1_h0", tag="wgt_once2")
+        xg1 = quantise(grouped1[:, half(0), :], codes1_h0[:], "xg1_h0")
+        xg2 = quantise(grouped_h0[:], codes2[:, half(0)], "xg2_h0")
+        xg2 = xg2 + quantise(grouped_h1[:], codes2[:, half(1)], "xg2_h1")
+        codes1_h1 = tile([P, HALF], U32, "codes1_h1", tag="grouped_h0")
+        xg1 = xg1 + quantise(grouped1[:, half(1), :], codes1_h1[:], "xg1_h1")
+        xg = [xg0, xg1, xg2]
 
         sums = {}
 
@@ -176,13 +167,24 @@ def tile_list_hboth_d_none_kernel(tc, xT, w4_words, w4_scales, c, u, wgt, wgo, o
             places = scatter_list[:, h * HALF // PER_COL : (h + 1) * HALF // PER_COL]
             nc.vector.tensor_tensor(placed[m][:].indirect(places), sums[m, h][:], wgo_sb[h][:], MULT)
 
-        for (j0, w), raw in zip(pieces, picked_last):
-            name = f"xg_last{j0}"
-            multiply(w4_pass(last), quantise(interleave(raw, w, name), w, name), j0, w, False, j0 < HALF)
+        for m in range(M // P):
+            for q in range(2):
+                multiply(m, q, u_mx[m], c_mx[q], start=True)
+        for m in range(M // P):
+            for a in range(PASSES):
+                for q in range(2):
+                    multiply(m, q, w4(a, m), xg[a][q], stop=a == last)
+        for m in range(M // P):
+            for a in range(PASSES):
+                for q in range(2, 4):
+                    multiply(m, q, w4(a, m), xg[a][q], start=a == 0)
         drain(0, 0)
-        grouped_c1 = interleave(c_raw[1], HALF, "c1")
         scatter(0, 0)
-        multiply(u_pass, quantise(grouped_c1, HALF, "c1"), HALF, HALF, False, True)
+        codes_c1 = tile([P, HALF], U32, "codes_c1")
+        c_mx = c_mx + quantise(interleave(c_raw[1][:], HALF, "c1")[:], codes_c1[:], "c1")
+        for m in range(M // P):
+            for q in range(2, 4):
+                multiply(m, q, u_mx[m], c_mx[q], stop=True)
         drain(1, 0, tag="c_raw1")
         scatter(1, 0)
         for m in range(M // P):

from contextlib import ExitStack

import concourse.mybir as mybir

K, M, T, S = 1536, 256, 1024, 512
L = 512
FLOPS = 2 * (K + L) * M * S

F32 = mybir.dt.float32
BF16 = mybir.dt.bfloat16
I32 = mybir.dt.int32
U32 = mybir.dt.uint32
U16 = mybir.dt.uint16
U8 = mybir.dt.uint8
FP8X4 = mybir.dt.float8_e4m3fn_x4
FP4X4 = mybir.dt.float4_e2m1fn_x4
MULT = mybir.AluOpType.mult

P = 128
PACK = 4
K_PASS = P * PACK
PASSES = K // K_PASS
HALF = S // 2
QUARTER = S // 4
PER_COL = 16


def tile_list_hboth_d_none_kernel(tc, xT, w4_words, w4_scales, c, u, wgt, wgo, offs, offs2, out):
    nc = tc.nc
    with ExitStack() as ctx:
        keep = ctx.enter_context(tc.tile_pool(name="keep", bufs=1))
        psum = ctx.enter_context(tc.psum_pool(name="psum", bufs=1))

        def tile(shape, dtype, name, tag=None):
            return keep.tile(shape, dtype, name=name, tag=tag or name, align_bytes=64)

        gather_list = keep.tile([P, S // PER_COL], U16, name="gather_list")
        scatter_list = keep.tile([P, S // PER_COL], U16, name="scatter_list")
        planes = [[tile([P, T], F32, f"plane{a}_{i}") for i in range(PACK)] for a in range(PASSES)]
        wgt_sb = tile([P, S], F32, "wgt_sb")
        wgt_once = [tile([P, w], F32, f"wgt_once{n}") for n, w in enumerate((HALF, HALF, QUARTER))]
        wgo_sb = [tile([P, HALF], F32, f"wgo{h}") for h in range(2)]
        c_raw = [tile([P, PACK, HALF], F32, f"c_raw{h}") for h in range(2)]
        u_raw = tile([P, PACK, M], F32, "u_raw")
        w_words = tile([P, PASSES, 2 * M], U8, "w_words")
        w_scales = tile([P, PASSES, M], U8, "w_scales")
        placed = [tile([P, T], F32, f"placed{m}") for m in range(M // P)]
        banks = [[psum.tile([P, QUARTER], F32, name=f"bank{m}_{q}") for q in range(4)] for m in range(M // P)]

        nc.vector.memset(w_scales[:].rearrange("p a n -> p (a n)").bitcast(I32), 0)
        for m in range(M // P):
            nc.vector.memset(placed[m][:], 0.0)

        x_planes = xT.rearrange("(a p i) t -> a i p t", p=P, i=PACK)
        c_rows = c.rearrange("(p i) j -> p i j", i=PACK)

        def load_planes(a, which):
            for i in which:
                nc.sync.dma_start(out=planes[a][i][:], in_=x_planes[a, i])

        def half(h):
            return slice(h * HALF, (h + 1) * HALF)

        load_planes(0, [0])
        nc.sync.dma_start(out=wgt_sb[:], in_=wgt)
        nc.sync.dma_start(gather_list[:], offs)
        load_planes(0, [1, 2, 3])
        load_planes(1, [0])
        nc.sync.dma_start(out=u_raw[:], in_=u.rearrange("(p i) n -> p i n", i=PACK))
        load_planes(1, [1])
        nc.sync.dma_start(out=c_raw[0][:], in_=c_rows[:, :, half(0)])
        load_planes(1, [2, 3])
        load_planes(2, range(PACK))
        nc.sync.dma_start(out=w_words[:].bitcast(I32), in_=w4_words.rearrange("a p b -> p a b").bitcast(I32))
        nc.sync.dma_start(out=wgo_sb[0][:], in_=wgo[:, half(0)])
        nc.sync.dma_start(scatter_list[:], offs2)
        nc.sync.dma_start(out=c_raw[1][:], in_=c_rows[:, :, half(1)])
        nc.sync.dma_start(out=wgo_sb[1][:], in_=wgo[:, half(1)])
        for quad in range(4):
            nc.scalar.dma_start(
                out=w_scales[32 * quad : 32 * quad + 4].bitcast(I32),
                in_=w4_scales[:, 4 * quad : 4 * quad + 4, :].rearrange("a r n -> r a n").bitcast(I32),
            )

        for copy in wgt_once:
            nc.scalar.copy(out=copy[:], in_=wgt_sb[:, : copy.shape[1]])

        def gather(a, i, j0, width, dst, weights=None):
            weights = wgt_sb[:, j0 : j0 + width] if weights is None else weights[:]
            picks = gather_list[:, j0 // PER_COL : (j0 + width) // PER_COL]
            nc.vector.tensor_tensor(dst, planes[a][i][:].indirect(picks), weights, MULT)

        def interleave_into(copy, grouped, raw):
            copy(out=grouped.rearrange("p (b e) i -> p b i e", e=4), in_=raw.rearrange("p i (b e) -> p b i e", e=4))

        def interleave(raw, width, name):
            grouped = tile([P, width, PACK], BF16, name + "_grouped")
            interleave_into(nc.scalar.copy, grouped[:], raw)
            return grouped

        def quantise(grouped, codes, name):
            scales = tile([P, codes.shape[1]], U8, name + "_scales")
            nc.vector.quantize_mx(out=codes.bitcast(FP8X4), scales=scales[:], in_=grouped.rearrange("p w i -> p (w i)"))
            return [
                (codes[:, q0 : q0 + QUARTER].bitcast(FP8X4), scales[:, q0 : q0 + QUARTER])
                for q0 in range(0, codes.shape[1], QUARTER)
            ]

        def multiply(m, q, lhs, rhs, start=False, stop=False):
            nc.tensor.matmul_mx(
                out=banks[m][q][:], lhsT=lhs[0], lhsT_scale=lhs[1], rhs=rhs[0], rhs_scale=rhs[1], start=start, stop=stop
            )

        def w4(a, m):
            return w_words[:, a, 2 * P * m : 2 * P * (m + 1)].bitcast(FP4X4), w_scales[:, a, P * m : P * (m + 1)]

        last = PASSES - 1
        picked = [tile([P, PACK, S], F32, f"picked{a}") for a in range(last)]
        picked_last = [tile([P, PACK, HALF], F32, f"picked_last{h}") for h in range(2)]

        for i in range(PACK):
            for h in range(2):
                gather(0, i, h * HALF, HALF, picked[0][:, i, half(h)])
        grouped0 = interleave(picked[0][:], S, "xg0")
        grouped_u = interleave(u_raw[:], M, "u")
        for i in range(PACK):
            gather(1, i, 0, HALF, picked[1][:, i, half(0)], wgt_once[i - 1] if i in (1, 2) else None)
            gather(1, i, HALF, HALF, picked[1][:, i, half(1)])
            if i == 1:
                codes0 = tile([P, S + M], U32, "codes0", tag="wgt_once0")
                xg0 = quantise(grouped0[:], codes0[:, :S], "xg0")
                u_mx = quantise(grouped_u[:], codes0[:, S:], "u")
            if i == 2:
                codes_c0 = tile([P, HALF], U32, "codes_c0", tag="wgt_once1")
                c_mx = quantise(interleave(c_raw[0][:], HALF, "c0")[:], codes_c0[:], "c0")
        grouped1 = interleave(picked[1][:], S, "xg1")
        for i in range(PACK - 1):
            for h in range(2):
                gather(last, i, h * HALF, HALF, picked_last[h][:, i, :])
        gather(last, 3, 0, QUARTER, picked_last[0][:, 3, :QUARTER], wgt_once[2])
        gather(last, 3, QUARTER, QUARTER, picked_last[0][:, 3, QUARTER:])
        gather(last, 3, HALF, HALF, picked_last[1][:, 3, :])

        grouped_h0 = tile([P, HALF, PACK], BF16, "grouped_h0")
        interleave_into(nc.scalar.copy, grouped_h0[:, :QUARTER, :], picked_last[0][:, :, :QUARTER])
        interleave_into(nc.vector.tensor_copy, grouped_h0[:, QUARTER:, :], picked_last[0][:, :, QUARTER:])
        grouped_h1 = interleave(picked_last[1][:], HALF, "xg2_h1")
        codes2 = tile([P, S], U32, "codes2")
        codes1_h0 = tile([P, HALF], U32, "codes1_h0", tag="wgt_once2")
        xg1 = quantise(grouped1[:, half(0), :], codes1_h0[:], "xg1_h0")
        xg2 = quantise(grouped_h0[:], codes2[:, half(0)], "xg2_h0")
        xg2 = xg2 + quantise(grouped_h1[:], codes2[:, half(1)], "xg2_h1")
        codes1_h1 = tile([P, HALF], U32, "codes1_h1", tag="grouped_h0")
        xg1 = xg1 + quantise(grouped1[:, half(1), :], codes1_h1[:], "xg1_h1")
        xg = [xg0, xg1, xg2]

        sums = {}

        def drain(m, h, tag=None):
            sums[m, h] = tile([P, HALF], F32, f"sums{m}_{h}", tag=tag)
            for q_in in range(2):
                nc.scalar.copy(
                    out=sums[m, h][:, q_in * QUARTER : (q_in + 1) * QUARTER], in_=banks[m][2 * h + q_in][:]
                )

        def scatter(m, h):
            places = scatter_list[:, h * HALF // PER_COL : (h + 1) * HALF // PER_COL]
            nc.vector.tensor_tensor(placed[m][:].indirect(places), sums[m, h][:], wgo_sb[h][:], MULT)

        for m in range(M // P):
            for q in range(2):
                multiply(m, q, u_mx[m], c_mx[q], start=True)
        for m in range(M // P):
            for a in range(PASSES):
                for q in range(2):
                    multiply(m, q, w4(a, m), xg[a][q], stop=a == last)
        for m in range(M // P):
            for a in range(PASSES):
                for q in range(2, 4):
                    multiply(m, q, w4(a, m), xg[a][q], start=a == 0)
        drain(0, 0)
        scatter(0, 0)
        codes_c1 = tile([P, HALF], U32, "codes_c1")
        c_mx = c_mx + quantise(interleave(c_raw[1][:], HALF, "c1")[:], codes_c1[:], "c1")
        for m in range(M // P):
            for q in range(2, 4):
                multiply(m, q, u_mx[m], c_mx[q], stop=True)
        drain(1, 0, tag="c_raw1")
        scatter(1, 0)
        for m in range(M // P):
            drain(m, 1)
            scatter(m, 1)
            nc.sync.dma_start(out=out[m * P : (m + 1) * P, :], in_=placed[m][:])
